import numpy as np
import ml_dtypes


def mxq(x, axis, fmt="e4m3"):
    dtype, down = {"e4m3": (ml_dtypes.float8_e4m3fn, 7), "e5m2": (ml_dtypes.float8_e5m2, 14)}[fmt]
    v = np.moveaxis(np.asarray(x, np.float32).astype(ml_dtypes.bfloat16).astype(np.float64), axis, -1)
    blocks = v.reshape(v.shape[:-1] + (-1, 32))
    amax = np.abs(blocks).max(-1, keepdims=True)
    byte = np.maximum(np.where(amax > 0, np.frexp(amax)[1] - 1 + 127, 0) - down, 1)
    scale = np.exp2(byte - 127.0)
    codes = (blocks / scale).astype(np.float32).astype(dtype).astype(np.float64)
    return np.moveaxis((codes * scale).reshape(v.shape), -1, axis)


WIDE = False


def mx_kscale(k):
    if not WIDE:
        return np.ones(k)
    levels = np.array([10, -10, 5, -5, 0])
    if k % 512:
        return np.exp2(np.random.permutation(np.resize(levels, k // 32))).repeat(32)
    a = np.empty((k // 512, 16))
    for p in range(k // 512):
        a[p, :8] = np.random.permutation(np.resize(levels, 8))
        for g in range(8):
            far = levels[np.abs(levels - a[p, g]) >= 10]
            a[p, g + 8] = far[np.random.randint(len(far))]
    return np.exp2(a.ravel()).repeat(32)


def f64(x):
    return np.asarray(x).astype(np.float64)


def striped(idx):
    return np.tile(idx.reshape(-1, 16).T, (8, 1)).astype(np.uint16)


def unstriped(offs):
    return offs[:16].T.reshape(-1).astype(np.int64)


def striped8(idx):
    return np.concatenate([x.reshape(-1, 16).T for x in idx]).astype(np.uint16)


def runs(offs, k):
    lists = np.stack([offs[16 * r : 16 * r + 16].T.reshape(-1) for r in range(8)]).astype(np.int64)
    return lists[np.arange(k) % 512 // 64]


def pack_weight(w):
    k, n = w.shape
    w = f64(np.asarray(w, np.float32).astype(ml_dtypes.bfloat16)).reshape(k // 32, 32, n)
    amax = np.abs(w).max(1)
    byte = np.clip(np.where(amax > 0, np.frexp(amax)[1] - 1 + 127 - 7, 1), 1, 254)
    scaled = (w * np.exp2(127.0 - byte)[:, None, :]).reshape(k, n).astype(np.float32)
    words = np.ascontiguousarray(scaled.reshape(k // 512, 128, 4, n).transpose(0, 1, 3, 2)).astype(ml_dtypes.float8_e4m3fn).view(np.uint8)
    return words, np.ascontiguousarray(byte.astype(np.uint8).reshape(k // 512, 16, n))


def unpack_weight(words, scales):
    g, p, n, _ = words.shape
    vals = np.ascontiguousarray(words).view(ml_dtypes.float8_e4m3fn).astype(np.float64) * np.repeat(np.exp2(scales.astype(np.float64) - 127.0), 8, axis=1)[..., None]
    return vals.transpose(0, 1, 3, 2).reshape(g * 512, n)


def relu(v):
    return np.maximum(v, 0.0)


K, T, S, V, N, H = 512, 2048, 512, 256, 512, 512


def setup_inputs():
    n = np.random.standard_normal
    s = mx_kscale(K)[:, None]
    u = mx_kscale(H)
    packed_xT = pack_weight(n((K, T)) * s)
    return {
        "x_words": packed_xT[0],
        "x_scales": packed_xT[1],
        "w1": (n((K, H)) / np.sqrt(K) / s).astype(np.float32),
        "w2": (n((K, H)) / np.sqrt(K) / s).astype(np.float32),
        "rad": np.repeat(np.random.uniform(0.5, 2.0, (8, V)), 64, axis=0).astype(np.float32),
        "gn": (np.random.uniform(0.5, 1.5, (H, 1)) * u[:, None]).astype(np.float32),
        "w3": (n((H, N)) / np.sqrt(H) / u[:, None]).astype(np.float32),
        "offs": striped(np.random.permutation(T)[:S]),
        "two": striped(np.random.permutation(T)[:S]),
        "b1": striped8(np.stack([np.random.permutation(S)[:V] for _ in range(8)])),
        "b2": striped8(np.stack([np.random.permutation(S)[:V] for _ in range(8)])),
    }


def reference(x_words, x_scales, w1, w2, rad, gn, w3, offs, two, b1, b2):
    xq = unpack_weight(x_words, x_scales)[:, unstriped(offs)]
    y = mxq(f64(w1), 0, "e4m3").T @ xq
    d = y[np.arange(H)[:, None], runs(b1, H)] - (y[np.arange(H)[:, None], runs(b2, H)])
    ov = relu(f64(rad) - np.abs(d))
    x_two = unpack_weight(x_words, x_scales)[:, unstriped(two)]
    c = mxq(f64(w2), 0, "e4m3").T @ x_two
    z = f64(gn) * ((ov / (np.abs(d) + 0.25)) * (d + 0.5 * (c[np.arange(H)[:, None], runs(b1, H)] - (c[np.arange(H)[:, None], runs(b2, H)]))))
    return mxq(f64(w3), 0, "e4m3").T @ mxq(z, 0, "e4m3")

@@ -1,0 +1,178 @@
+from contextlib import ExitStack
+
+import concourse.mybir as mybir
+
+K, T, S, V, N, H = 512, 2048, 512, 256, 512, 512
+FLOPS = 2 * K * H * S * 2 + 2 * H * N * V
+
+F32 = mybir.dt.float32
+BF16 = mybir.dt.bfloat16
+I32 = mybir.dt.int32
+U32 = mybir.dt.uint32
+U16 = mybir.dt.uint16
+U8 = mybir.dt.uint8
+FP8X4 = mybir.dt.float8_e4m3fn_x4
+ALU = mybir.AluOpType
+ACT = mybir.ActivationFunctionType
+
+P = 128
+PACK = 4
+HALF = 256
+
+
+def tile_picked_contactf_none_p_kernel(tc, x_words, x_scales, w1, w2, rad, gn, w3, offs, two, b1, b2, out):
+    nc = tc.nc
+    with ExitStack() as ctx:
+        sb = ctx.enter_context(tc.tile_pool(name="sb", bufs=1))
+        psum = ctx.enter_context(tc.psum_pool(name="psum", bufs=1))
+
+        def tile(name, shape, dtype):
+            return sb.tile(shape, dtype, name=name, align_bytes=64)
+
+        def load_list(name, src):
+            lst = sb.tile(list(src.shape), U16, name=name)
+            nc.sync.dma_start(lst[:], src)
+            return lst
+
+        def load_weight(name, w):
+            rows = w.rearrange("(p j) c -> p j c", j=PACK)
+            halves = []
+            for h in range(2):
+                raw = tile(f"{name}_raw{h}", [P, PACK, HALF], F32)
+                nc.sync.dma_start(raw[:], rows[:, :, h * HALF : (h + 1) * HALF])
+                halves.append(raw)
+            return halves
+
+        def cast(engine, grouped, halves, m0, m1):
+            h = m0 // 64
+            src = halves[h][:].rearrange("p j (m t) -> p m j t", t=PACK)[:, m0 - 64 * h : m1 - 64 * h]
+            dst = grouped[:, :, m0:m1, :].rearrange("p t m j -> p m j t")
+            if engine == "scalar":
+                nc.scalar.copy(dst, src)
+            else:
+                nc.vector.tensor_copy(dst, src)
+
+        def quantize(codes, scales, src):
+            nc.vector.quantize_mx(out=codes.bitcast(FP8X4), scales=scales, in_=src)
+
+        def product(acc, w_codes, w_scales, t, m_codes, m_scales):
+            cols = slice(t * P, (t + 1) * P)
+            nc.tensor.matmul_mx(out=acc, lhsT=w_codes[:, cols].bitcast(FP8X4), lhsT_scale=w_scales[:, cols],
+                                rhs=m_codes.bitcast(FP8X4), rhs_scale=m_scales, start=True, stop=True)
+
+        offs_t = load_list("offs_t", offs)
+        table_scales = tile("table_scales", [P, T], U8)
+        for q in range(4):
+            rows = x_scales[0, 4 * q : 4 * q + 4, :].bitcast(I32).unsqueeze(0).broadcast_to([8, 4, T // 4])
+            (nc.sync if q % 2 == 0 else nc.scalar).dma_start(table_scales[32 * q : 32 * q + 32, :].bitcast(I32), rows)
+        table_words = tile("table_words", [P, T], U32)
+        nc.sync.dma_start(table_words[:].bitcast(I32), x_words[0].rearrange("p n r -> p (n r)").bitcast(I32))
+        two_t = load_list("two_t", two)
+        gain = tile("gain", [P, PACK], F32)
+        nc.sync.dma_start(gain[:], gn.rearrange("(p t) o -> p (t o)", t=PACK))
+        radius = tile("radius", [P, V], F32)
+        nc.sync.dma_start(radius[:], rad.rearrange("(p t) v -> p t v", t=PACK)[:, 0, :])
+        w1_raw = load_weight("w1", w1)
+        b2_t = load_list("b2_t", b2)
+        b1_t = load_list("b1_t", b1)
+        w2_raw = load_weight("w2", w2)
+        w3_raw = load_weight("w3", w3)
+
+        picked = []
+        for name, lst in (("pos", offs_t), ("vel", two_t)):
+            scales = tile(f"{name}_scales", [P, S], U8)
+            nc.vector.tensor_copy(scales[:], table_scales[:].indirect(lst[:]))
+            picked.append([None, scales])
+        for i, (name, lst) in enumerate((("pos", offs_t), ("vel", two_t))):
+            words = tile(f"{name}_words", [P, S], U32)
+            nc.vector.tensor_copy(words[:], table_words[:].indirect(lst[:]))
+            picked[i][0] = words
+
+        sign = tile("sign", [P, PACK], F32)
+        nc.scalar.activation(sign[:], gain[:], ACT.Sign)
+        half_sign = tile("half_sign", [P, PACK], F32)
+        nc.scalar.activation(half_sign[:], sign[:], ACT.Copy, scale=0.5)
+        size = tile("size", [P, PACK], F32)
+        nc.scalar.activation(size[:], gain[:], ACT.Abs)
+        neg_size = tile("neg_size", [P, PACK], F32)
+        nc.scalar.activation(neg_size[:], size[:], ACT.Copy, scale=-1.0)
+        reach = tile("reach", [P, PACK, V], F32)
+        for t in range(PACK):
+            nc.scalar.activation(reach[:, t, :], radius[:], ACT.Copy, scale=size[:, t : t + 1])
+
+        grouped = [tile(f"w{i}_bf", [P, PACK, P, PACK], BF16) for i in range(3)]
+        codes = [tile(f"w{i}_codes", [P, H], U32) for i in range(3)]
+        planes = [tile(f"w{i}_scales", [P, H], U8) for i in range(3)]
+
+        cast("scalar", grouped[0], w1_raw, 0, 64)
+        cast("scalar", grouped[0], w1_raw, 64, 96)
+        cast("vector", grouped[0], w1_raw, 96, 128)
+        y_bank = [psum.tile([P, S], F32, name=f"y_bank{t}", tag=f"bank{t}") for t in range(PACK)]
+        for t in range(PACK):
+            cols = slice(t * P, (t + 1) * P)
+            quantize(codes[0][:, cols], planes[0][:, cols], grouped[0][:, t].rearrange("p m j -> p (m j)"))
+            product(y_bank[t][:], codes[0], planes[0], t, picked[0][0][:], picked[0][1][:])
+
+        cast("vector", grouped[1], w2_raw, 0, 64)
+        cast("vector", grouped[1], w2_raw, 64, 128)
+        y = [tile(f"y{t}", [P, S], F32) for t in range(PACK)]
+        y_second = tile("y_second", [P, PACK, V], F32)
+        d = tile("d", [P, PACK, V], F32)
+        for t in range(PACK):
+            nc.scalar.activation(y[t][:], y_bank[t][:], ACT.Copy, scale=sign[:, t : t + 1])
+            nc.scalar.activation(y_second[:, t, :], y[t][:].indirect(b2_t[:]), ACT.Copy)
+        quantize(codes[1][:], planes[1][:], grouped[1][:].rearrange("p t m j -> p (t m j)"))
+        c_bank = [psum.tile([P, S], F32, name=f"c_bank{t}", tag=f"bank{PACK + t}") for t in range(PACK)]
+        for t in range(PACK):
+            product(c_bank[t][:], codes[1], planes[1], t, picked[1][0][:], picked[1][1][:])
+        e = [tile(f"e{t}", [P, S], F32) for t in range(PACK)]
+        for t in range(PACK):
+            nc.vector.tensor_tensor(d[:, t, :], y[t][:].indirect(b1_t[:]), y_second[:, t, :], ALU.subtract)
+            nc.vector.scalar_tensor_tensor(e[t][:], c_bank[t][:], half_sign[:, t : t + 1], y[t][:], ALU.mult, ALU.add)
+
+        dist = tile("dist", [P, PACK, V], F32)
+        root = tile("root", [P, PACK, V], F32)
+        recip = tile("recip", [P, PACK, V], F32)
+        gap = tile("gap", [P, PACK, V], F32)
+        force = tile("force", [P, PACK, V], F32)
+        e_second = tile("e_second", [P, PACK, V], F32)
+        s = tile("s", [P, PACK, V], F32)
+        for u in range(2):
+            ts = slice(2 * u, 2 * u + 2)
+            nc.scalar.activation(dist[:, ts], d[:, ts], ACT.Abs)
+            nc.scalar.activation(root[:, ts], dist[:, ts], ACT.Abs_reciprocal_sqrt, bias=0.25)
+            nc.scalar.activation(recip[:, ts], root[:, ts], ACT.Square)
+            cast("scalar", grouped[2], w3_raw, 64 * u, 64 * u + 64)
+            for t in range(2 * u, 2 * u + 2):
+                nc.scalar.activation(e_second[:, t, :], e[t][:].indirect(b2_t[:]), ACT.Copy)
+            for t in range(2 * u, 2 * u + 2):
+                nc.vector.scalar_tensor_tensor(gap[:, t, :], dist[:, t, :], neg_size[:, t : t + 1], reach[:, t, :], ALU.mult, ALU.add)
+            flat = lambda a: a[:, ts].rearrange("p t v -> p (t v)")
+            nc.vector.scalar_tensor_tensor(flat(force), flat(gap), 0.0, flat(recip), ALU.max, ALU.mult)
+            if u == 1:
+                quantize(codes[2][:], planes[2][:], grouped[2][:].rearrange("p t m j -> p (t m j)"))
+            for t in range(2 * u, 2 * u + 2):
+                nc.vector.tensor_tensor(s[:, t, :], e[t][:].indirect(b1_t[:]), e_second[:, t, :], ALU.subtract)
+
+        out_rows = out.rearrange("(p t) v -> p t v", t=PACK)
+        z = [tile(f"z{h}", [P, P, PACK], BF16) for h in range(2)]
+        for h in range(2):
+            vs = slice(h * P, (h + 1) * P)
+            nc.vector.tensor_tensor(z[h][:].rearrange("p (c i) t -> p c t i", i=4), force[:, :, vs].rearrange("p t (c i) -> p c t i", i=4),
+                                    s[:, :, vs].rearrange("p t (c i) -> p c t i", i=4), ALU.mult)
+        for h in range(2):
+            vs = slice(h * P, (h + 1) * P)
+            z_codes = tile(f"z_codes{h}", [P, P], U32)
+            z_scales = tile(f"z_scales{h}", [P, P], U8)
+            quantize(z_codes[:], z_scales[:], z[h][:].rearrange("p v t -> p (v t)"))
+            for u in range(2):
+                bank = psum.tile([P, S], F32, name=f"o_bank{h}{u}", tag=f"bank{2 * h + u}")
+                for k in range(2):
+                    product(bank[:, k * P : (k + 1) * P], codes[2], planes[2], 2 * u + k, z_codes[:], z_scales[:])
+                res = tile(f"res{h}{u}", [P, 2, P], F32)
+                flat_res = res[:].rearrange("p k v -> p (k v)")
+                if h == 1 and u == 1:
+                    nc.vector.tensor_copy(flat_res, bank[:, 0 : 2 * P])
+                else:
+                    nc.scalar.copy(flat_res, bank[:, 0 : 2 * P])
+                nc.sync.dma_start(out_rows[:, 2 * u : 2 * u + 2, vs], res[:])

@@ -17,7 +17,6 @@ ACT = mybir.ActivationFunctionType
 
 P = 128
 PACK = 4
-HALF = 256
 
 
 def tile_picked_contactf_none_p_kernel(tc, x_words, x_scales, w1, w2, rad, gn, w3, offs, two, b1, b2, out):
@@ -26,8 +25,8 @@ def tile_picked_contactf_none_p_kernel(tc, x_words, x_scales, w1, w2, rad, gn, w
         sb = ctx.enter_context(tc.tile_pool(name="sb", bufs=1))
         psum = ctx.enter_context(tc.psum_pool(name="psum", bufs=1))
 
-        def tile(name, shape, dtype):
-            return sb.tile(shape, dtype, name=name, align_bytes=64)
+        def tile(name, shape, dtype, tag=None):
+            return sb.tile(shape, dtype, name=name, tag=tag or name, align_bytes=64)
 
         def load_list(name, src):
             lst = sb.tile(list(src.shape), U16, name=name)
@@ -35,25 +34,18 @@ def tile_picked_contactf_none_p_kernel(tc, x_words, x_scales, w1, w2, rad, gn, w
             return lst
 
         def load_weight(name, w):
-            rows = w.rearrange("(p j) c -> p j c", j=PACK)
-            halves = []
-            for h in range(2):
-                raw = tile(f"{name}_raw{h}", [P, PACK, HALF], F32)
-                nc.sync.dma_start(raw[:], rows[:, :, h * HALF : (h + 1) * HALF])
-                halves.append(raw)
-            return halves
+            raw = tile(name, [P, PACK, H], F32)
+            nc.sync.dma_start(raw[:], w.rearrange("(p j) c -> p j c", j=PACK))
+            return raw
 
-        def cast(engine, grouped, halves, m0, m1):
-            h = m0 // 64
-            src = halves[h][:].rearrange("p j (m t) -> p m j t", t=PACK)[:, m0 - 64 * h : m1 - 64 * h]
-            dst = grouped[:, :, m0:m1, :].rearrange("p t m j -> p m j t")
-            if engine == "scalar":
-                nc.scalar.copy(dst, src)
-            else:
-                nc.vector.tensor_copy(dst, src)
+        def cast_dealt(copy, grouped, raw, m0, m1):
+            copy(grouped[:].rearrange("p (t m) j -> p m t j", t=PACK)[:, m0:m1], raw[:].rearrange("p j (m t) -> p m t j", t=PACK)[:, m0:m1])
+
+        def cast_plain(copy, grouped, raw, c0, c1):
+            copy(grouped[:, c0:c1, :], raw[:, :, c0:c1].rearrange("p j c -> p c j"))
 
         def quantize(codes, scales, src):
-            nc.vector.quantize_mx(out=codes.bitcast(FP8X4), scales=scales, in_=src)
+            nc.vector.quantize_mx(out=codes[:].bitcast(FP8X4), scales=scales[:], in_=src[:].rearrange("p c j -> p (c j)"))
 
         def product(acc, w_codes, w_scales, t, m_codes, m_scales):
             cols = slice(t * P, (t + 1) * P)
@@ -65,28 +57,44 @@ def tile_picked_contactf_none_p_kernel(tc, x_words, x_scales, w1, w2, rad, gn, w
         for q in range(4):
             rows = x_scales[0, 4 * q : 4 * q + 4, :].bitcast(I32).unsqueeze(0).broadcast_to([8, 4, T // 4])
             (nc.sync if q % 2 == 0 else nc.scalar).dma_start(table_scales[32 * q : 32 * q + 32, :].bitcast(I32), rows)
-        table_words = tile("table_words", [P, T], U32)
-        nc.sync.dma_start(table_words[:].bitcast(I32), x_words[0].rearrange("p n r -> p (n r)").bitcast(I32))
-        two_t = load_list("two_t", two)
         gain = tile("gain", [P, PACK], F32)
         nc.sync.dma_start(gain[:], gn.rearrange("(p t) o -> p (t o)", t=PACK))
         radius = tile("radius", [P, V], F32)
         nc.sync.dma_start(radius[:], rad.rearrange("(p t) v -> p t v", t=PACK)[:, 0, :])
-        w1_raw = load_weight("w1", w1)
+        w1_raw = load_weight("w1_raw", w1)
+        two_t = load_list("two_t", two)
+        table_words = tile("table_words", [P, T], U32)
+        nc.sync.dma_start(table_words[:].bitcast(I32), x_words[0].rearrange("p n r -> p (n r)").bitcast(I32))
         b2_t = load_list("b2_t", b2)
         b1_t = load_list("b1_t", b1)
-        w2_raw = load_weight("w2", w2)
-        w3_raw = load_weight("w3", w3)
+        w2_raw = load_weight("w2_raw", w2)
+        w3_raw = load_weight("w3_raw", w3)
 
-        picked = []
-        for name, lst in (("pos", offs_t), ("vel", two_t)):
-            scales = tile(f"{name}_scales", [P, S], U8)
-            nc.vector.tensor_copy(scales[:], table_scales[:].indirect(lst[:]))
-            picked.append([None, scales])
-        for i, (name, lst) in enumerate((("pos", offs_t), ("vel", two_t))):
-            words = tile(f"{name}_words", [P, S], U32)
-            nc.vector.tensor_copy(words[:], table_words[:].indirect(lst[:]))
-            picked[i][0] = words
+        warm = tile("warm", [P, 1], F32)
+        nc.vector.memset(warm[:], 1.0)
+        warm_out = tile("warm_out", [P, 1], F32)
+        nc.scalar.activation(warm_out[:], warm[:], ACT.Abs_reciprocal_sqrt)
+
+        grouped = [tile(f"w{i}_bf", [P, H, PACK], BF16) for i in range(3)]
+        codes = [tile(f"w{i}_codes", [P, H], U32) for i in range(3)]
+        planes = [tile(f"w{i}_scales", [P, H], U8) for i in range(3)]
+        picked_words = [tile(f"picked_words{i}", [P, S], U32) for i in range(2)]
+        picked_scales = [tile(f"picked_scales{i}", [P, S], U8) for i in range(2)]
+
+        nc.vector.tensor_copy(picked_scales[0][:], table_scales[:].indirect(offs_t[:]))
+        nc.vector.tensor_copy(picked_scales[1][:], table_scales[:].indirect(two_t[:]))
+        cast_dealt(nc.scalar.copy, grouped[0], w1_raw, 0, 64)
+        cast_dealt(nc.vector.tensor_copy, grouped[0], w1_raw, 64, 128)
+        quantize(codes[0], planes[0], grouped[0])
+        y_bank = [psum.tile([P, S], F32, name=f"y_bank{t}", tag=f"bank{t}") for t in range(PACK)]
+        halves = [slice(0, S // 2), slice(S // 2, S)]
+        for h in range(2):
+            nc.vector.tensor_copy(picked_words[0][:, halves[h]], table_words[:].indirect(offs_t[:, 16 * h : 16 * h + 16]))
+        for u in range(2):
+            for h in range(2):
+                for t in range(2 * u, 2 * u + 2):
+                    product(y_bank[t][:, halves[h]], codes[0], planes[0], t, picked_words[0][:, halves[h]], picked_scales[0][:, halves[h]])
+        nc.vector.tensor_copy(picked_words[1][:], table_words[:].indirect(two_t[:]))
 
         sign = tile("sign", [P, PACK], F32)
         nc.scalar.activation(sign[:], gain[:], ACT.Sign)
@@ -100,71 +108,69 @@ def tile_picked_contactf_none_p_kernel(tc, x_words, x_scales, w1, w2, rad, gn, w
         for t in range(PACK):
             nc.scalar.activation(reach[:, t, :], radius[:], ACT.Copy, scale=size[:, t : t + 1])
 
-        grouped = [tile(f"w{i}_bf", [P, PACK, P, PACK], BF16) for i in range(3)]
-        codes = [tile(f"w{i}_codes", [P, H], U32) for i in range(3)]
-        planes = [tile(f"w{i}_scales", [P, H], U8) for i in range(3)]
-
-        cast("scalar", grouped[0], w1_raw, 0, 64)
-        cast("scalar", grouped[0], w1_raw, 64, 96)
-        cast("vector", grouped[0], w1_raw, 96, 128)
-        y_bank = [psum.tile([P, S], F32, name=f"y_bank{t}", tag=f"bank{t}") for t in range(PACK)]
-        for t in range(PACK):
-            cols = slice(t * P, (t + 1) * P)
-            quantize(codes[0][:, cols], planes[0][:, cols], grouped[0][:, t].rearrange("p m j -> p (m j)"))
-            product(y_bank[t][:], codes[0], planes[0], t, picked[0][0][:], picked[0][1][:])
-
-        cast("vector", grouped[1], w2_raw, 0, 64)
-        cast("vector", grouped[1], w2_raw, 64, 128)
         y = [tile(f"y{t}", [P, S], F32) for t in range(PACK)]
         y_second = tile("y_second", [P, PACK, V], F32)
-        d = tile("d", [P, PACK, V], F32)
         for t in range(PACK):
             nc.scalar.activation(y[t][:], y_bank[t][:], ACT.Copy, scale=sign[:, t : t + 1])
             nc.scalar.activation(y_second[:, t, :], y[t][:].indirect(b2_t[:]), ACT.Copy)
-        quantize(codes[1][:], planes[1][:], grouped[1][:].rearrange("p t m j -> p (t m j)"))
+        cast_dealt(nc.vector.tensor_copy, grouped[1], w2_raw, 0, 128)
+        quantize(codes[1], planes[1], grouped[1])
         c_bank = [psum.tile([P, S], F32, name=f"c_bank{t}", tag=f"bank{PACK + t}") for t in range(PACK)]
         for t in range(PACK):
-            product(c_bank[t][:], codes[1], planes[1], t, picked[1][0][:], picked[1][1][:])
+            product(c_bank[t][:], codes[1], planes[1], t, picked_words[1][:], picked_scales[1][:])
         e = [tile(f"e{t}", [P, S], F32) for t in range(PACK)]
-        for t in range(PACK):
-            nc.vector.tensor_tensor(d[:, t, :], y[t][:].indirect(b1_t[:]), y_second[:, t, :], ALU.subtract)
-            nc.vector.scalar_tensor_tensor(e[t][:], c_bank[t][:], half_sign[:, t : t + 1], y[t][:], ALU.mult, ALU.add)
-
+        d = [tile("d01", [P, 2, V], F32, tag="w1_bf"), tile("d23", [P, 2, V], F32, tag="w2_raw")]
         dist = tile("dist", [P, PACK, V], F32)
-        root = tile("root", [P, PACK, V], F32)
-        recip = tile("recip", [P, PACK, V], F32)
         gap = tile("gap", [P, PACK, V], F32)
-        force = tile("force", [P, PACK, V], F32)
         e_second = tile("e_second", [P, PACK, V], F32)
         s = tile("s", [P, PACK, V], F32)
-        for u in range(2):
-            ts = slice(2 * u, 2 * u + 2)
-            nc.scalar.activation(dist[:, ts], d[:, ts], ACT.Abs)
-            nc.scalar.activation(root[:, ts], dist[:, ts], ACT.Abs_reciprocal_sqrt, bias=0.25)
-            nc.scalar.activation(recip[:, ts], root[:, ts], ACT.Square)
-            cast("scalar", grouped[2], w3_raw, 64 * u, 64 * u + 64)
-            for t in range(2 * u, 2 * u + 2):
-                nc.scalar.activation(e_second[:, t, :], e[t][:].indirect(b2_t[:]), ACT.Copy)
-            for t in range(2 * u, 2 * u + 2):
-                nc.vector.scalar_tensor_tensor(gap[:, t, :], dist[:, t, :], neg_size[:, t : t + 1], reach[:, t, :], ALU.mult, ALU.add)
-            flat = lambda a: a[:, ts].rearrange("p t v -> p (t v)")
-            nc.vector.scalar_tensor_tensor(flat(force), flat(gap), 0.0, flat(recip), ALU.max, ALU.mult)
-            if u == 1:
-                quantize(codes[2][:], planes[2][:], grouped[2][:].rearrange("p t m j -> p (t m j)"))
-            for t in range(2 * u, 2 * u + 2):
-                nc.vector.tensor_tensor(s[:, t, :], e[t][:].indirect(b1_t[:]), e_second[:, t, :], ALU.subtract)
 
-        out_rows = out.rearrange("(p t) v -> p t v", t=PACK)
-        z = [tile(f"z{h}", [P, P, PACK], BF16) for h in range(2)]
+        def position_difference(t):
+            nc.vector.tensor_tensor(d[t // 2][:, t % 2, :], y[t][:].indirect(b1_t[:]), y_second[:, t, :], ALU.subtract)
+
+        def add_speed(t):
+            nc.vector.scalar_tensor_tensor(e[t][:], c_bank[t][:], half_sign[:, t : t + 1], y[t][:], ALU.mult, ALU.add)
+
+        for t in range(3):
+            position_difference(t)
+        add_speed(0)
+        add_speed(1)
+        position_difference(3)
+        add_speed(2)
+        add_speed(3)
+        for u in range(2):
+            nc.scalar.activation(e_second[:, 2 * u, :], e[2 * u][:].indirect(b2_t[:]), ACT.Copy)
+            nc.scalar.activation(dist[:, 2 * u : 2 * u + 2, :], d[u][:], ACT.Abs)
+            nc.scalar.activation(e_second[:, 2 * u + 1, :], e[2 * u + 1][:].indirect(b2_t[:]), ACT.Copy)
+        for t in range(PACK):
+            nc.vector.tensor_tensor(s[:, t, :], e[t][:].indirect(b1_t[:]), e_second[:, t, :], ALU.subtract)
+            nc.vector.scalar_tensor_tensor(gap[:, t, :], dist[:, t, :], neg_size[:, t : t + 1], reach[:, t, :], ALU.mult, ALU.add)
+        recip = []
         for h in range(2):
             vs = slice(h * P, (h + 1) * P)
-            nc.vector.tensor_tensor(z[h][:].rearrange("p (c i) t -> p c t i", i=4), force[:, :, vs].rearrange("p t (c i) -> p c t i", i=4),
-                                    s[:, :, vs].rearrange("p t (c i) -> p c t i", i=4), ALU.mult)
+            root = tile(f"root{h}", [P, P, PACK], F32)
+            nc.scalar.activation(root[:], dist[:, :, vs].rearrange("p t v -> p v t"), ACT.Abs_reciprocal_sqrt, bias=0.25)
+            recip.append(tile(f"recip{h}", [P, P, PACK], F32))
+            nc.scalar.activation(recip[h][:], root[:], ACT.Square)
+            if h == 0:
+                cast_plain(nc.scalar.copy, grouped[2], w3_raw, 0, 256)
+                cast_plain(nc.scalar.copy, grouped[2], w3_raw, 256, 512)
+
+        out_rows = out.rearrange("(t p) v -> p t v", t=PACK)
+        z = []
+        for h in range(2):
+            vs = slice(h * P, (h + 1) * P)
+            push = tile(f"push{h}", [P, PACK, P], F32)
+            nc.vector.scalar_tensor_tensor(push[:], gap[:, :, vs], 0.0, s[:, :, vs], ALU.max, ALU.mult)
+            if h == 1:
+                quantize(codes[2], planes[2], grouped[2])
+            z.append(tile(f"z{h}", [P, P, PACK], BF16))
+            nc.vector.tensor_tensor(z[h][:], push[:].rearrange("p t v -> p v t"), recip[h][:], ALU.mult)
         for h in range(2):
             vs = slice(h * P, (h + 1) * P)
             z_codes = tile(f"z_codes{h}", [P, P], U32)
             z_scales = tile(f"z_scales{h}", [P, P], U8)
-            quantize(z_codes[:], z_scales[:], z[h][:].rearrange("p v t -> p (v t)"))
+            quantize(z_codes, z_scales, z[h])
             for u in range(2):
                 bank = psum.tile([P, S], F32, name=f"o_bank{h}{u}", tag=f"bank{2 * h + u}")
                 for k in range(2):

from contextlib import ExitStack

import concourse.mybir as mybir

K, T, S, V, N, H = 512, 2048, 512, 256, 512, 512
FLOPS = 2 * K * H * S * 2 + 2 * H * N * V

F32 = mybir.dt.float32
BF16 = mybir.dt.bfloat16
I32 = mybir.dt.int32
U32 = mybir.dt.uint32
U16 = mybir.dt.uint16
U8 = mybir.dt.uint8
FP8X4 = mybir.dt.float8_e4m3fn_x4
ALU = mybir.AluOpType
ACT = mybir.ActivationFunctionType

P = 128
PACK = 4


def tile_picked_contactf_none_p_kernel(tc, x_words, x_scales, w1, w2, rad, gn, w3, offs, two, b1, b2, out):
    nc = tc.nc
    with ExitStack() as ctx:
        sb = ctx.enter_context(tc.tile_pool(name="sb", bufs=1))
        psum = ctx.enter_context(tc.psum_pool(name="psum", bufs=1))

        def tile(name, shape, dtype, tag=None):
            return sb.tile(shape, dtype, name=name, tag=tag or name, align_bytes=64)

        def load_list(name, src):
            lst = sb.tile(list(src.shape), U16, name=name)
            nc.sync.dma_start(lst[:], src)
            return lst

        def load_weight(name, w):
            raw = tile(name, [P, PACK, H], F32)
            nc.sync.dma_start(raw[:], w.rearrange("(p j) c -> p j c", j=PACK))
            return raw

        def cast_dealt(copy, grouped, raw, m0, m1):
            copy(grouped[:].rearrange("p (t m) j -> p m t j", t=PACK)[:, m0:m1], raw[:].rearrange("p j (m t) -> p m t j", t=PACK)[:, m0:m1])

        def cast_plain(copy, grouped, raw, c0, c1):
            copy(grouped[:, c0:c1, :], raw[:, :, c0:c1].rearrange("p j c -> p c j"))

        def quantize(codes, scales, src):
            nc.vector.quantize_mx(out=codes[:].bitcast(FP8X4), scales=scales[:], in_=src[:].rearrange("p c j -> p (c j)"))

        def product(acc, w_codes, w_scales, t, m_codes, m_scales):
            cols = slice(t * P, (t + 1) * P)
            nc.tensor.matmul_mx(out=acc, lhsT=w_codes[:, cols].bitcast(FP8X4), lhsT_scale=w_scales[:, cols],
                                rhs=m_codes.bitcast(FP8X4), rhs_scale=m_scales, start=True, stop=True)

        offs_t = load_list("offs_t", offs)
        table_scales = tile("table_scales", [P, T], U8)
        for q in range(4):
            rows = x_scales[0, 4 * q : 4 * q + 4, :].bitcast(I32).unsqueeze(0).broadcast_to([8, 4, T // 4])
            (nc.sync if q % 2 == 0 else nc.scalar).dma_start(table_scales[32 * q : 32 * q + 32, :].bitcast(I32), rows)
        gain = tile("gain", [P, PACK], F32)
        nc.sync.dma_start(gain[:], gn.rearrange("(p t) o -> p (t o)", t=PACK))
        radius = tile("radius", [P, V], F32)
        nc.sync.dma_start(radius[:], rad.rearrange("(p t) v -> p t v", t=PACK)[:, 0, :])
        w1_raw = load_weight("w1_raw", w1)
        two_t = load_list("two_t", two)
        table_words = tile("table_words", [P, T], U32)
        nc.sync.dma_start(table_words[:].bitcast(I32), x_words[0].rearrange("p n r -> p (n r)").bitcast(I32))
        b2_t = load_list("b2_t", b2)
        b1_t = load_list("b1_t", b1)
        w2_raw = load_weight("w2_raw", w2)
        w3_raw = load_weight("w3_raw", w3)

        warm = tile("warm", [P, 1], F32)
        nc.vector.memset(warm[:], 1.0)
        warm_out = tile("warm_out", [P, 1], F32)
        nc.scalar.activation(warm_out[:], warm[:], ACT.Abs_reciprocal_sqrt)

        grouped = [tile(f"w{i}_bf", [P, H, PACK], BF16) for i in range(3)]
        codes = [tile(f"w{i}_codes", [P, H], U32) for i in range(3)]
        planes = [tile(f"w{i}_scales", [P, H], U8) for i in range(3)]
        picked_words = [tile(f"picked_words{i}", [P, S], U32) for i in range(2)]
        picked_scales = [tile(f"picked_scales{i}", [P, S], U8) for i in range(2)]

        nc.vector.tensor_copy(picked_scales[0][:], table_scales[:].indirect(offs_t[:]))
        nc.vector.tensor_copy(picked_scales[1][:], table_scales[:].indirect(two_t[:]))
        cast_dealt(nc.scalar.copy, grouped[0], w1_raw, 0, 64)
        cast_dealt(nc.vector.tensor_copy, grouped[0], w1_raw, 64, 128)
        quantize(codes[0], planes[0], grouped[0])
        y_bank = [psum.tile([P, S], F32, name=f"y_bank{t}", tag=f"bank{t}") for t in range(PACK)]
        halves = [slice(0, S // 2), slice(S // 2, S)]
        for h in range(2):
            nc.vector.tensor_copy(picked_words[0][:, halves[h]], table_words[:].indirect(offs_t[:, 16 * h : 16 * h + 16]))
        for u in range(2):
            for h in range(2):
                for t in range(2 * u, 2 * u + 2):
                    product(y_bank[t][:, halves[h]], codes[0], planes[0], t, picked_words[0][:, halves[h]], picked_scales[0][:, halves[h]])
        nc.vector.tensor_copy(picked_words[1][:], table_words[:].indirect(two_t[:]))

        sign = tile("sign", [P, PACK], F32)
        nc.scalar.activation(sign[:], gain[:], ACT.Sign)
        half_sign = tile("half_sign", [P, PACK], F32)
        nc.scalar.activation(half_sign[:], sign[:], ACT.Copy, scale=0.5)
        size = tile("size", [P, PACK], F32)
        nc.scalar.activation(size[:], gain[:], ACT.Abs)
        neg_size = tile("neg_size", [P, PACK], F32)
        nc.scalar.activation(neg_size[:], size[:], ACT.Copy, scale=-1.0)
        reach = tile("reach", [P, PACK, V], F32)
        for t in range(PACK):
            nc.scalar.activation(reach[:, t, :], radius[:], ACT.Copy, scale=size[:, t : t + 1])

        y = [tile(f"y{t}", [P, S], F32) for t in range(PACK)]
        y_second = tile("y_second", [P, PACK, V], F32)
        for t in range(PACK):
            nc.scalar.activation(y[t][:], y_bank[t][:], ACT.Copy, scale=sign[:, t : t + 1])
            nc.scalar.activation(y_second[:, t, :], y[t][:].indirect(b2_t[:]), ACT.Copy)
        cast_dealt(nc.vector.tensor_copy, grouped[1], w2_raw, 0, 128)
        quantize(codes[1], planes[1], grouped[1])
        c_bank = [psum.tile([P, S], F32, name=f"c_bank{t}", tag=f"bank{PACK + t}") for t in range(PACK)]
        for t in range(PACK):
            product(c_bank[t][:], codes[1], planes[1], t, picked_words[1][:], picked_scales[1][:])
        e = [tile(f"e{t}", [P, S], F32) for t in range(PACK)]
        d = [tile("d01", [P, 2, V], F32, tag="w1_bf"), tile("d23", [P, 2, V], F32, tag="w2_raw")]
        dist = tile("dist", [P, PACK, V], F32)
        gap = tile("gap", [P, PACK, V], F32)
        e_second = tile("e_second", [P, PACK, V], F32)
        s = tile("s", [P, PACK, V], F32)

        def position_difference(t):
            nc.vector.tensor_tensor(d[t // 2][:, t % 2, :], y[t][:].indirect(b1_t[:]), y_second[:, t, :], ALU.subtract)

        def add_speed(t):
            nc.vector.scalar_tensor_tensor(e[t][:], c_bank[t][:], half_sign[:, t : t + 1], y[t][:], ALU.mult, ALU.add)

        for t in range(3):
            position_difference(t)
        add_speed(0)
        add_speed(1)
        position_difference(3)
        add_speed(2)
        add_speed(3)
        for u in range(2):
            nc.scalar.activation(e_second[:, 2 * u, :], e[2 * u][:].indirect(b2_t[:]), ACT.Copy)
            nc.scalar.activation(dist[:, 2 * u : 2 * u + 2, :], d[u][:], ACT.Abs)
            nc.scalar.activation(e_second[:, 2 * u + 1, :], e[2 * u + 1][:].indirect(b2_t[:]), ACT.Copy)
        for t in range(PACK):
            nc.vector.tensor_tensor(s[:, t, :], e[t][:].indirect(b1_t[:]), e_second[:, t, :], ALU.subtract)
            nc.vector.scalar_tensor_tensor(gap[:, t, :], dist[:, t, :], neg_size[:, t : t + 1], reach[:, t, :], ALU.mult, ALU.add)
        recip = []
        for h in range(2):
            vs = slice(h * P, (h + 1) * P)
            root = tile(f"root{h}", [P, P, PACK], F32)
            nc.scalar.activation(root[:], dist[:, :, vs].rearrange("p t v -> p v t"), ACT.Abs_reciprocal_sqrt, bias=0.25)
            recip.append(tile(f"recip{h}", [P, P, PACK], F32))
            nc.scalar.activation(recip[h][:], root[:], ACT.Square)
            if h == 0:
                cast_plain(nc.scalar.copy, grouped[2], w3_raw, 0, 256)
                cast_plain(nc.scalar.copy, grouped[2], w3_raw, 256, 512)

        out_rows = out.rearrange("(t p) v -> p t v", t=PACK)
        z = []
        for h in range(2):
            vs = slice(h * P, (h + 1) * P)
            push = tile(f"push{h}", [P, PACK, P], F32)
            nc.vector.scalar_tensor_tensor(push[:], gap[:, :, vs], 0.0, s[:, :, vs], ALU.max, ALU.mult)
            if h == 1:
                quantize(codes[2], planes[2], grouped[2])
            z.append(tile(f"z{h}", [P, P, PACK], BF16))
            nc.vector.tensor_tensor(z[h][:], push[:].rearrange("p t v -> p v t"), recip[h][:], ALU.mult)
        for h in range(2):
            vs = slice(h * P, (h + 1) * P)
            z_codes = tile(f"z_codes{h}", [P, P], U32)
            z_scales = tile(f"z_scales{h}", [P, P], U8)
            quantize(z_codes, z_scales, z[h])
            for u in range(2):
                bank = psum.tile([P, S], F32, name=f"o_bank{h}{u}", tag=f"bank{2 * h + u}")
                for k in range(2):
                    product(bank[:, k * P : (k + 1) * P], codes[2], planes[2], 2 * u + k, z_codes[:], z_scales[:])
                res = tile(f"res{h}{u}", [P, 2, P], F32)
                flat_res = res[:].rearrange("p k v -> p (k v)")
                if h == 1 and u == 1:
                    nc.vector.tensor_copy(flat_res, bank[:, 0 : 2 * P])
                else:
                    nc.scalar.copy(flat_res, bank[:, 0 : 2 * P])
                nc.sync.dma_start(out_rows[:, 2 * u : 2 * u + 2, vs], res[:])
